import numpy as np, ml_dtypes
CORES = [2,10,34,50,74,82,98,114,130,138,162,178,202,210,226,242]
N = 16
W, KW, DIL = 1024, 3, 4
H = (KW // 2) * DIL
def setup_inputs(rng):
    return {"x": rng.standard_normal((N, 128, W), dtype=np.float32).astype(ml_dtypes.bfloat16), "w": rng.standard_normal((N, 128, KW * 128), dtype=np.float32).astype(ml_dtypes.bfloat16)}
def setup_inputs_big(rng):
    d = setup_inputs(rng)
    for k in ("x", "w"): d[k] = (d[k].astype(np.float32) * 1024.0).astype(d[k].dtype)
    return d
def setup_inputs_small(rng):
    d = setup_inputs(rng)
    for k in ("x", "w"): d[k] = (d[k].astype(np.float32) * (1 / 1024.0)).astype(d[k].dtype)
    return d
def reference(x, w):
    X, W_ = x.astype(np.float64), w.astype(np.float64)
    g = np.concatenate(list(X), axis=1)
    p = np.pad(g, ((0, 0), (H, H)))
    y = np.zeros((N, 128, W))
    for r in range(N):
        for i in range(KW):
            y[r] += W_[r][:, 128 * i:128 * i + 128].T @ p[:, W * r + i * DIL:W * r + i * DIL + W]
    return {"y": y.astype(ml_dtypes.bfloat16 if x.dtype != np.float64 else np.float64)}

@@ -1,0 +1,122 @@
+from concourse.bass import DstId, RemoteDMATransfer
+
+CH = 128
+WID = 1024
+HALO = 4
+CUT = 512
+BANK = 512
+
+SCRATCH = {
+    "sendL": ("dram", [CH, HALO], "bfloat16"),
+    "sendR": ("dram", [CH, HALO], "bfloat16"),
+    "landL": ("dram", [CH, HALO], "bfloat16"),
+    "landR": ("dram", [CH, HALO], "bfloat16"),
+    "halo": ("sbuf", [CH, 2 * HALO], "bfloat16"),
+    "ws": ("sbuf", [CH, 3 * CH], "bfloat16"),
+    "xs": ("sbuf", [CH, WID], "bfloat16"),
+    "y0": ("sbuf", [CH, CUT - 2 * HALO], "bfloat16"),
+    "y1": ("sbuf", [CH, WID - CUT], "bfloat16"),
+    "ye": ("sbuf", [CH, 2 * HALO], "bfloat16"),
+    "pA": ("psum", [CH, BANK], "float32"),
+    "pB": ("psum", [CH, BANK], "float32"),
+    "pE": ("psum", [CH, 2 * BANK], "float32"),
+}
+SEMAPHORES = ["ld_edge", "sent", "arrL", "arrR", "ld_w", "ld_x0", "ld_x1", "ld_hL", "ld_hR",
+              "mm0", "mm1", "mme", "cp0", "cp1", "cpe", "st_a", "st_b"]
+
+
+def _engines(mask, n, used):
+    out = 0
+    for b in range(mask.bit_length()):
+        bit = 1 << b
+        if n and (mask & bit) and not (used & bit):
+            out |= bit
+            n -= 1
+    return out
+
+
+def rank_program(g, core, T, topo):
+    rank = T.rank_of(core)
+    if rank is None:
+        return
+    S = T.sem
+    n_ranks = len(T.cores)
+    left = T.cores[rank - 1] if rank > 0 else None
+    right = T.cores[rank + 1] if rank + 1 < n_ranks else None
+    qa, qb = g.sync, g.scalar
+    w = [T.ws[:, CH * i:CH * (i + 1)] for i in range(3)]
+
+    if left is not None:
+        qa.dma_start(T.sendL[:, :], T.x[:, 0:HALO]).then_inc(S.ld_edge, 16)
+    if right is not None:
+        qb.dma_start(T.sendR[:, :], T.x[:, WID - HALO:WID]).then_inc(S.ld_edge, 16)
+    qa.dma_start(T.ws[:, :], T.w[:, :]).then_inc(S.ld_w, 16)
+    qb.dma_start(T.xs[:, 0:CUT], T.x[:, 0:CUT]).then_inc(S.ld_x0, 16)
+    qa.dma_start(T.xs[:, CUT:WID], T.x[:, CUT:WID]).then_inc(S.ld_x1, 16)
+
+    transfers, used = [], 0
+    for dst, src_ap, dst_ap, sem in ((left, T.sendL, T.landR, S.arrR), (right, T.sendR, T.landL, S.arrL)):
+        if dst is None:
+            continue
+        rid, pid = topo.addr(dst, core)
+        m = _engines(topo.mask(core, dst), 1, used)
+        used |= m
+        transfers.append(RemoteDMATransfer(dst_ids=[DstId(rid=rid, pnc=pid)], dma_engine_mask=m, remote_sem=sem,
+                                           src=src_ap[:, :], dst=dst_ap[:, :]))
+    g.wait_ge(S.ld_edge, 16 * len(transfers))
+    g.remote_dma_fused(transfers, local_sem=S.sent)
+    g.wait_ge(S.sent, len(transfers))
+
+    te = g.tensor
+    eL = T.pE[:, BANK - HALO:BANK]
+    eR = T.pE[:, BANK:BANK + HALO]
+    n0, n1 = CUT - 2 * HALO, WID - CUT
+    te.wait_ge(S.ld_w, 16)
+    te.wait_ge(S.ld_x0, 16)
+    for i in range(3):
+        mm = te.matmul(T.pA[:, 0:n0], w[i], T.xs[:, HALO * i:HALO * i + n0], start=(i == 0), stop=(i == 2))
+    mm.then_inc(S.mm0, 1)
+    te.matmul(eL, w[1], T.xs[:, 0:HALO], start=True, stop=False)
+    mm = te.matmul(eL, w[2], T.xs[:, HALO:2 * HALO], start=False, stop=(left is None))
+    if left is None:
+        mm.then_inc(S.mme, 1)
+    te.wait_ge(S.ld_x1, 16)
+    for i in range(3):
+        a = n0 + HALO * i
+        mm = te.matmul(T.pB[:, 0:n1], w[i], T.xs[:, a:a + n1], start=(i == 0), stop=(i == 2))
+    mm.then_inc(S.mm1, 1)
+    te.matmul(eR, w[0], T.xs[:, WID - 2 * HALO:WID - HALO], start=True, stop=False)
+    mm = te.matmul(eR, w[1], T.xs[:, WID - HALO:WID], start=False, stop=(right is None))
+    if right is None:
+        mm.then_inc(S.mme, 1)
+    if left is not None:
+        te.wait_ge(S.ld_hL, 16)
+        te.matmul(eL, w[0], T.halo[:, 0:HALO], start=False, stop=True).then_inc(S.mme, 1)
+    if right is not None:
+        te.wait_ge(S.ld_hR, 16)
+        te.matmul(eR, w[2], T.halo[:, HALO:2 * HALO], start=False, stop=True).then_inc(S.mme, 1)
+
+    ve = g.vector
+    ve.wait_ge(S.mm0, 1)
+    ve.tensor_copy(T.y0[:, :], T.pA[:, 0:n0]).then_inc(S.cp0, 1)
+    ve.wait_ge(S.mm1, 1)
+    ve.tensor_copy(T.y1[:, :], T.pB[:, 0:n1]).then_inc(S.cp1, 1)
+    ve.wait_ge(S.mme, 2)
+    ve.tensor_copy(T.ye[:, :], T.pE[:, BANK - HALO:BANK + HALO]).then_inc(S.cpe, 1)
+
+    qa.wait_ge(S.cp0, 1)
+    qa.dma_start(T.y[:, HALO:HALO + n0], T.y0[:, :]).then_inc(S.st_a, 16)
+    qb.wait_ge(S.cp1, 1)
+    qb.dma_start(T.y[:, HALO + n0:WID - HALO], T.y1[:, :]).then_inc(S.st_b, 16)
+    if left is not None:
+        qa.wait_ge(S.arrL, 1)
+        qa.dma_start(T.halo[:, 0:HALO], T.landL[:, :]).then_inc(S.ld_hL, 16)
+    if right is not None:
+        qb.wait_ge(S.arrR, 1)
+        qb.dma_start(T.halo[:, HALO:2 * HALO], T.landR[:, :]).then_inc(S.ld_hR, 16)
+    qa.wait_ge(S.cpe, 1)
+    qa.dma_start(T.y[:, 0:HALO], T.ye[:, 0:HALO]).then_inc(S.st_a, 16)
+    qb.wait_ge(S.cpe, 1)
+    qb.dma_start(T.y[:, WID - HALO:WID], T.ye[:, HALO:2 * HALO]).then_inc(S.st_b, 16)
+    qa.wait_ge(S.st_a, 32)
+    qb.wait_ge(S.st_b, 32)

@@ -3,36 +3,39 @@ from concourse.bass import DstId, RemoteDMATransfer
 CH = 128
 WID = 1024
 HALO = 4
-CUT = 512
+CUTS = [0, 256, 768, 1024]
+NP = len(CUTS) - 1
 BANK = 512
+HI = [CUTS[j + 1] - HALO for j in range(NP)]
+LO = [HALO] + HI[:-1]
 
 SCRATCH = {
     "sendL": ("dram", [CH, HALO], "bfloat16"),
     "sendR": ("dram", [CH, HALO], "bfloat16"),
     "landL": ("dram", [CH, HALO], "bfloat16"),
     "landR": ("dram", [CH, HALO], "bfloat16"),
-    "halo": ("sbuf", [CH, 2 * HALO], "bfloat16"),
+    "hL": ("sbuf", [CH, 2 * HALO], "bfloat16"),
+    "hR": ("sbuf", [CH, 2 * HALO], "bfloat16"),
+    "wqL": ("sbuf", [CH, 2 * CH], "bfloat16"),
+    "wqR": ("sbuf", [CH, 2 * CH], "bfloat16"),
+    "yeL": ("sbuf", [CH, 2 * HALO], "bfloat16"),
+    "yeR": ("sbuf", [CH, 2 * HALO], "bfloat16"),
     "ws": ("sbuf", [CH, 3 * CH], "bfloat16"),
     "xs": ("sbuf", [CH, WID], "bfloat16"),
-    "y0": ("sbuf", [CH, CUT - 2 * HALO], "bfloat16"),
-    "y1": ("sbuf", [CH, WID - CUT], "bfloat16"),
-    "ye": ("sbuf", [CH, 2 * HALO], "bfloat16"),
-    "pA": ("psum", [CH, BANK], "float32"),
-    "pB": ("psum", [CH, BANK], "float32"),
-    "pE": ("psum", [CH, 2 * BANK], "float32"),
+    "pL": ("psum", [CH, BANK], "float32"),
+    "pR": ("psum", [CH, BANK], "float32"),
 }
-SEMAPHORES = ["ld_edge", "sent", "arrL", "arrR", "ld_w", "ld_x0", "ld_x1", "ld_hL", "ld_hR",
-              "mm0", "mm1", "mme", "cp0", "cp1", "cpe", "st_a", "st_b"]
+SEMAPHORES = ["ld_edge", "sent", "arrL", "arrR", "ld_w", "ld_hL", "ld_hR", "ld_wq", "mmL", "mmR", "cpL", "cpR",
+              "st_a", "st_b"]
+for _j in range(NP):
+    SCRATCH["yc%d" % _j] = ("sbuf", [CH, HI[_j] - LO[_j]], "bfloat16")
+    SCRATCH["pc%d" % _j] = ("psum", [CH, BANK], "float32")
+    SEMAPHORES += ["ld_x%d" % _j, "mm%d" % _j, "cp%d" % _j]
 
 
-def _engines(mask, n, used):
-    out = 0
-    for b in range(mask.bit_length()):
-        bit = 1 << b
-        if n and (mask & bit) and not (used & bit):
-            out |= bit
-            n -= 1
-    return out
+def _engine(mask, k):
+    bits = [1 << b for b in range(mask.bit_length()) if (mask >> b) & 1]
+    return bits[0] if k == 0 else bits[-1]
 
 
 def rank_program(g, core, T, topo):
@@ -51,16 +54,24 @@ def rank_program(g, core, T, topo):
     if right is not None:
         qb.dma_start(T.sendR[:, :], T.x[:, WID - HALO:WID]).then_inc(S.ld_edge, 16)
     qa.dma_start(T.ws[:, :], T.w[:, :]).then_inc(S.ld_w, 16)
-    qb.dma_start(T.xs[:, 0:CUT], T.x[:, 0:CUT]).then_inc(S.ld_x0, 16)
-    qa.dma_start(T.xs[:, CUT:WID], T.x[:, CUT:WID]).then_inc(S.ld_x1, 16)
+    for j in range(NP):
+        q = qb if j % 2 == 0 else qa
+        q.dma_start(T.xs[:, CUTS[j]:CUTS[j + 1]], T.x[:, CUTS[j]:CUTS[j + 1]]).then_inc(S["ld_x%d" % j], 16)
+    HC = CH // 2
+    n_wq = 0
+    for nb, buf, tap in ((right, T.wqR, 2), (left, T.wqL, 0)):
+        if nb is None:
+            continue
+        for q, odd in ((qa, 0), (qb, 1)):
+            q.dma_start(buf[0:HC, CH * odd:CH * (odd + 1)], T.w[odd:CH:2, CH * tap:CH * (tap + 1)]).then_inc(S.ld_wq, 16)
+            n_wq += 16
 
-    transfers, used = [], 0
+    transfers = []
     for dst, src_ap, dst_ap, sem in ((left, T.sendL, T.landR, S.arrR), (right, T.sendR, T.landL, S.arrL)):
         if dst is None:
             continue
         rid, pid = topo.addr(dst, core)
-        m = _engines(topo.mask(core, dst), 1, used)
-        used |= m
+        m = _engine(topo.mask(core, dst), len(transfers))
         transfers.append(RemoteDMATransfer(dst_ids=[DstId(rid=rid, pnc=pid)], dma_engine_mask=m, remote_sem=sem,
                                            src=src_ap[:, :], dst=dst_ap[:, :]))
     g.wait_ge(S.ld_edge, 16 * len(transfers))
@@ -68,55 +79,56 @@ def rank_program(g, core, T, topo):
     g.wait_ge(S.sent, len(transfers))
 
     te = g.tensor
-    eL = T.pE[:, BANK - HALO:BANK]
-    eR = T.pE[:, BANK:BANK + HALO]
-    n0, n1 = CUT - 2 * HALO, WID - CUT
+    eL = T.pL[:, 0:HALO]
+    eR = T.pR[:, 0:HALO]
     te.wait_ge(S.ld_w, 16)
-    te.wait_ge(S.ld_x0, 16)
-    for i in range(3):
-        mm = te.matmul(T.pA[:, 0:n0], w[i], T.xs[:, HALO * i:HALO * i + n0], start=(i == 0), stop=(i == 2))
-    mm.then_inc(S.mm0, 1)
+    for j in range(NP):
+        te.wait_ge(S["ld_x%d" % j], 16)
+        n = HI[j] - LO[j]
+        for i in range(3):
+            a = LO[j] + HALO * (i - 1)
+            mm = te.matmul(T["pc%d" % j][:, 0:n], w[i], T.xs[:, a:a + n], start=(i == 0), stop=(i == 2))
+        mm.then_inc(S["mm%d" % j], 1)
     te.matmul(eL, w[1], T.xs[:, 0:HALO], start=True, stop=False)
     mm = te.matmul(eL, w[2], T.xs[:, HALO:2 * HALO], start=False, stop=(left is None))
     if left is None:
-        mm.then_inc(S.mme, 1)
-    te.wait_ge(S.ld_x1, 16)
-    for i in range(3):
-        a = n0 + HALO * i
-        mm = te.matmul(T.pB[:, 0:n1], w[i], T.xs[:, a:a + n1], start=(i == 0), stop=(i == 2))
-    mm.then_inc(S.mm1, 1)
+        mm.then_inc(S.mmL, 1)
     te.matmul(eR, w[0], T.xs[:, WID - 2 * HALO:WID - HALO], start=True, stop=False)
     mm = te.matmul(eR, w[1], T.xs[:, WID - HALO:WID], start=False, stop=(right is None))
     if right is None:
-        mm.then_inc(S.mme, 1)
-    if left is not None:
-        te.wait_ge(S.ld_hL, 16)
-        te.matmul(eL, w[0], T.halo[:, 0:HALO], start=False, stop=True).then_inc(S.mme, 1)
+        mm.then_inc(S.mmR, 1)
+    te.wait_ge(S.ld_wq, n_wq)
     if right is not None:
         te.wait_ge(S.ld_hR, 16)
-        te.matmul(eR, w[2], T.halo[:, HALO:2 * HALO], start=False, stop=True).then_inc(S.mme, 1)
+        te.matmul(eR, T.wqR[0:HC, 0:CH], T.hR[0:HC, 0:HALO], start=False, stop=False)
+        te.matmul(eR, T.wqR[0:HC, CH:2 * CH], T.hR[0:HC, HALO:2 * HALO], start=False, stop=True).then_inc(S.mmR, 1)
+    if left is not None:
+        te.wait_ge(S.ld_hL, 16)
+        te.matmul(eL, T.wqL[0:HC, 0:CH], T.hL[0:HC, 0:HALO], start=False, stop=False)
+        te.matmul(eL, T.wqL[0:HC, CH:2 * CH], T.hL[0:HC, HALO:2 * HALO], start=False, stop=True).then_inc(S.mmL, 1)
 
     ve = g.vector
-    ve.wait_ge(S.mm0, 1)
-    ve.tensor_copy(T.y0[:, :], T.pA[:, 0:n0]).then_inc(S.cp0, 1)
-    ve.wait_ge(S.mm1, 1)
-    ve.tensor_copy(T.y1[:, :], T.pB[:, 0:n1]).then_inc(S.cp1, 1)
-    ve.wait_ge(S.mme, 2)
-    ve.tensor_copy(T.ye[:, :], T.pE[:, BANK - HALO:BANK + HALO]).then_inc(S.cpe, 1)
+    for j in range(NP):
+        ve.wait_ge(S["mm%d" % j], 1)
+        ve.tensor_copy(T["yc%d" % j][:, :], T["pc%d" % j][:, 0:HI[j] - LO[j]]).then_inc(S["cp%d" % j], 1)
+    ve.wait_ge(S.mmR, 1)
+    ve.tensor_copy(T.yeR[:, 0:HALO], eR).then_inc(S.cpR, 1)
+    ve.wait_ge(S.mmL, 1)
+    ve.tensor_copy(T.yeL[:, 0:HALO], eL).then_inc(S.cpL, 1)
 
-    qa.wait_ge(S.cp0, 1)
-    qa.dma_start(T.y[:, HALO:HALO + n0], T.y0[:, :]).then_inc(S.st_a, 16)
-    qb.wait_ge(S.cp1, 1)
-    qb.dma_start(T.y[:, HALO + n0:WID - HALO], T.y1[:, :]).then_inc(S.st_b, 16)
-    if left is not None:
-        qa.wait_ge(S.arrL, 1)
-        qa.dma_start(T.halo[:, 0:HALO], T.landL[:, :]).then_inc(S.ld_hL, 16)
+    for j in range(NP):
+        qa.wait_ge(S["cp%d" % j], 1)
+        qa.dma_start(T.y[:, LO[j]:HI[j]], T["yc%d" % j][:, :]).then_inc(S.st_a, 16)
+    qa.wait_ge(S.cpL, 1)
+    qa.dma_start(T.y[:, 0:HALO], T.yeL[:, 0:HALO]).then_inc(S.st_a, 16)
+    qa.wait_ge(S.st_a, 16 * (NP + 1))
+
     if right is not None:
         qb.wait_ge(S.arrR, 1)
-        qb.dma_start(T.halo[:, HALO:2 * HALO], T.landR[:, :]).then_inc(S.ld_hR, 16)
-    qa.wait_ge(S.cpe, 1)
-    qa.dma_start(T.y[:, 0:HALO], T.ye[:, 0:HALO]).then_inc(S.st_a, 16)
-    qb.wait_ge(S.cpe, 1)
-    qb.dma_start(T.y[:, WID - HALO:WID], T.ye[:, HALO:2 * HALO]).then_inc(S.st_b, 16)
-    qa.wait_ge(S.st_a, 32)
-    qb.wait_ge(S.st_b, 32)
+        qb.dma_start(T.hR[0:HC, :], T.landR[:, :]).then_inc(S.ld_hR, 16)
+    if left is not None:
+        qb.wait_ge(S.arrL, 1)
+        qb.dma_start(T.hL[0:HC, :], T.landL[:, :]).then_inc(S.ld_hL, 16)
+    qb.wait_ge(S.cpR, 1)
+    qb.dma_start(T.y[:, WID - HALO:WID], T.yeR[:, 0:HALO]).then_inc(S.st_b, 16)
+    qb.wait_ge(S.st_b, 16)

@@ -3,21 +3,17 @@ from concourse.bass import DstId, RemoteDMATransfer
 CH = 128
 WID = 1024
 HALO = 4
-CUTS = [0, 256, 768, 1024]
+CUTS = [0, 128, 384, 640, 896, 1024]
 NP = len(CUTS) - 1
 BANK = 512
 HI = [CUTS[j + 1] - HALO for j in range(NP)]
 LO = [HALO] + HI[:-1]
 
 SCRATCH = {
-    "sendL": ("dram", [CH, HALO], "bfloat16"),
-    "sendR": ("dram", [CH, HALO], "bfloat16"),
-    "landL": ("dram", [CH, HALO], "bfloat16"),
-    "landR": ("dram", [CH, HALO], "bfloat16"),
+    "sL": ("sbuf", [CH, 2 * HALO], "bfloat16"),
+    "sR": ("sbuf", [CH, 2 * HALO], "bfloat16"),
     "hL": ("sbuf", [CH, 2 * HALO], "bfloat16"),
     "hR": ("sbuf", [CH, 2 * HALO], "bfloat16"),
-    "wqL": ("sbuf", [CH, 2 * CH], "bfloat16"),
-    "wqR": ("sbuf", [CH, 2 * CH], "bfloat16"),
     "yeL": ("sbuf", [CH, 2 * HALO], "bfloat16"),
     "yeR": ("sbuf", [CH, 2 * HALO], "bfloat16"),
     "ws": ("sbuf", [CH, 3 * CH], "bfloat16"),
@@ -25,17 +21,17 @@ SCRATCH = {
     "pL": ("psum", [CH, BANK], "float32"),
     "pR": ("psum", [CH, BANK], "float32"),
 }
-SEMAPHORES = ["ld_edge", "sent", "arrL", "arrR", "ld_w", "ld_hL", "ld_hR", "ld_wq", "mmL", "mmR", "cpL", "cpR",
-              "st_a", "st_b"]
+SEMAPHORES = ["ld_edge", "sent", "arrL", "arrR", "ld_w", "mmL", "mmR", "cpL", "cpR", "st_a", "st_b"]
 for _j in range(NP):
     SCRATCH["yc%d" % _j] = ("sbuf", [CH, HI[_j] - LO[_j]], "bfloat16")
     SCRATCH["pc%d" % _j] = ("psum", [CH, BANK], "float32")
     SEMAPHORES += ["ld_x%d" % _j, "mm%d" % _j, "cp%d" % _j]
 
 
-def _engine(mask, k):
+def _half(mask, k):
     bits = [1 << b for b in range(mask.bit_length()) if (mask >> b) & 1]
-    return bits[0] if k == 0 else bits[-1]
+    n = len(bits) // 2
+    return sum(bits[0:n] if k == 0 else bits[n:2 * n]), n
 
 
 def rank_program(g, core, T, topo):
@@ -49,39 +45,41 @@ def rank_program(g, core, T, topo):
     qa, qb = g.sync, g.scalar
     w = [T.ws[:, CH * i:CH * (i + 1)] for i in range(3)]
 
-    if left is not None:
-        qa.dma_start(T.sendL[:, :], T.x[:, 0:HALO]).then_inc(S.ld_edge, 16)
-    if right is not None:
-        qb.dma_start(T.sendR[:, :], T.x[:, WID - HALO:WID]).then_inc(S.ld_edge, 16)
+    qa.dma_start(T.sL[:, :], T.x[:, 0:2 * HALO]).then_inc(S.ld_edge, 16)
+    qb.dma_start(T.sR[:, :], T.x[:, WID - 2 * HALO:WID]).then_inc(S.ld_edge, 16)
     qa.dma_start(T.ws[:, :], T.w[:, :]).then_inc(S.ld_w, 16)
     for j in range(NP):
         q = qb if j % 2 == 0 else qa
         q.dma_start(T.xs[:, CUTS[j]:CUTS[j + 1]], T.x[:, CUTS[j]:CUTS[j + 1]]).then_inc(S["ld_x%d" % j], 16)
-    HC = CH // 2
-    n_wq = 0
-    for nb, buf, tap in ((right, T.wqR, 2), (left, T.wqL, 0)):
-        if nb is None:
-            continue
-        for q, odd in ((qa, 0), (qb, 1)):
-            q.dma_start(buf[0:HC, CH * odd:CH * (odd + 1)], T.w[odd:CH:2, CH * tap:CH * (tap + 1)]).then_inc(S.ld_wq, 16)
-            n_wq += 16
 
-    transfers = []
-    for dst, src_ap, dst_ap, sem in ((left, T.sendL, T.landR, S.arrR), (right, T.sendR, T.landL, S.arrL)):
+    transfers, n_sent, n_arr = [], 0, {}
+    for side, dst, src_ap, dst_ap, sem in (("L", left, T.sL[:, 0:HALO], T.hR[:, 0:HALO], S.arrR),
+                                           ("R", right, T.sR[:, HALO:2 * HALO], T.hL[:, 0:HALO], S.arrL)):
         if dst is None:
             continue
         rid, pid = topo.addr(dst, core)
-        m = _engine(topo.mask(core, dst), len(transfers))
+        m, n = _half(topo.mask(core, dst), len(transfers))
+        n_sent += n
+        n_arr[side] = _half(topo.mask(dst, core), 0)[1]
         transfers.append(RemoteDMATransfer(dst_ids=[DstId(rid=rid, pnc=pid)], dma_engine_mask=m, remote_sem=sem,
-                                           src=src_ap[:, :], dst=dst_ap[:, :]))
-    g.wait_ge(S.ld_edge, 16 * len(transfers))
+                                           src=src_ap, dst=dst_ap))
+    g.wait_ge(S.ld_edge, 32)
     g.remote_dma_fused(transfers, local_sem=S.sent)
-    g.wait_ge(S.sent, len(transfers))
+    g.wait_ge(S.sent, n_sent)
 
     te = g.tensor
     eL = T.pL[:, 0:HALO]
     eR = T.pR[:, 0:HALO]
     te.wait_ge(S.ld_w, 16)
+    te.wait_ge(S.ld_edge, 32)
+    te.matmul(eL, w[1], T.sL[:, 0:HALO], start=True, stop=False)
+    mm = te.matmul(eL, w[2], T.sL[:, HALO:2 * HALO], start=False, stop=(left is None))
+    if left is None:
+        mm.then_inc(S.mmL, 1)
+    te.matmul(eR, w[0], T.sR[:, 0:HALO], start=True, stop=False)
+    mm = te.matmul(eR, w[1], T.sR[:, HALO:2 * HALO], start=False, stop=(right is None))
+    if right is None:
+        mm.then_inc(S.mmR, 1)
     for j in range(NP):
         te.wait_ge(S["ld_x%d" % j], 16)
         n = HI[j] - LO[j]
@@ -89,23 +87,12 @@ def rank_program(g, core, T, topo):
             a = LO[j] + HALO * (i - 1)
             mm = te.matmul(T["pc%d" % j][:, 0:n], w[i], T.xs[:, a:a + n], start=(i == 0), stop=(i == 2))
         mm.then_inc(S["mm%d" % j], 1)
-    te.matmul(eL, w[1], T.xs[:, 0:HALO], start=True, stop=False)
-    mm = te.matmul(eL, w[2], T.xs[:, HALO:2 * HALO], start=False, stop=(left is None))
-    if left is None:
-        mm.then_inc(S.mmL, 1)
-    te.matmul(eR, w[0], T.xs[:, WID - 2 * HALO:WID - HALO], start=True, stop=False)
-    mm = te.matmul(eR, w[1], T.xs[:, WID - HALO:WID], start=False, stop=(right is None))
-    if right is None:
-        mm.then_inc(S.mmR, 1)
-    te.wait_ge(S.ld_wq, n_wq)
     if right is not None:
-        te.wait_ge(S.ld_hR, 16)
-        te.matmul(eR, T.wqR[0:HC, 0:CH], T.hR[0:HC, 0:HALO], start=False, stop=False)
-        te.matmul(eR, T.wqR[0:HC, CH:2 * CH], T.hR[0:HC, HALO:2 * HALO], start=False, stop=True).then_inc(S.mmR, 1)
+        te.wait_ge(S.arrR, n_arr["R"])
+        te.matmul(eR, w[2], T.hR[:, 0:HALO], start=False, stop=True).then_inc(S.mmR, 1)
     if left is not None:
-        te.wait_ge(S.ld_hL, 16)
-        te.matmul(eL, T.wqL[0:HC, 0:CH], T.hL[0:HC, 0:HALO], start=False, stop=False)
-        te.matmul(eL, T.wqL[0:HC, CH:2 * CH], T.hL[0:HC, HALO:2 * HALO], start=False, stop=True).then_inc(S.mmL, 1)
+        te.wait_ge(S.arrL, n_arr["L"])
+        te.matmul(eL, w[0], T.hL[:, 0:HALO], start=False, stop=True).then_inc(S.mmL, 1)
 
     ve = g.vector
     for j in range(NP):
@@ -116,19 +103,15 @@ def rank_program(g, core, T, topo):
     ve.wait_ge(S.mmL, 1)
     ve.tensor_copy(T.yeL[:, 0:HALO], eL).then_inc(S.cpL, 1)
 
+    n_st = {"a": 0, "b": 0}
     for j in range(NP):
-        qa.wait_ge(S["cp%d" % j], 1)
-        qa.dma_start(T.y[:, LO[j]:HI[j]], T["yc%d" % j][:, :]).then_inc(S.st_a, 16)
-    qa.wait_ge(S.cpL, 1)
-    qa.dma_start(T.y[:, 0:HALO], T.yeL[:, 0:HALO]).then_inc(S.st_a, 16)
-    qa.wait_ge(S.st_a, 16 * (NP + 1))
-
-    if right is not None:
-        qb.wait_ge(S.arrR, 1)
-        qb.dma_start(T.hR[0:HC, :], T.landR[:, :]).then_inc(S.ld_hR, 16)
-    if left is not None:
-        qb.wait_ge(S.arrL, 1)
-        qb.dma_start(T.hL[0:HC, :], T.landL[:, :]).then_inc(S.ld_hL, 16)
+        q, key = (qa, "a") if j % 2 == 0 else (qb, "b")
+        q.wait_ge(S["cp%d" % j], 1)
+        q.dma_start(T.y[:, LO[j]:HI[j]], T["yc%d" % j][:, :]).then_inc(S["st_" + key], 16)
+        n_st[key] += 16
     qb.wait_ge(S.cpR, 1)
     qb.dma_start(T.y[:, WID - HALO:WID], T.yeR[:, 0:HALO]).then_inc(S.st_b, 16)
-    qb.wait_ge(S.st_b, 16)
+    qa.wait_ge(S.cpL, 1)
+    qa.dma_start(T.y[:, 0:HALO], T.yeL[:, 0:HALO]).then_inc(S.st_a, 16)
+    qa.wait_ge(S.st_a, n_st["a"] + 16)
+    qb.wait_ge(S.st_b, n_st["b"] + 16)

from concourse.bass import DstId, RemoteDMATransfer

CH = 128
WID = 1024
HALO = 4
CUTS = [0, 128, 384, 640, 896, 1024]
NP = len(CUTS) - 1
BANK = 512
HI = [CUTS[j + 1] - HALO for j in range(NP)]
LO = [HALO] + HI[:-1]

SCRATCH = {
    "sL": ("sbuf", [CH, 2 * HALO], "bfloat16"),
    "sR": ("sbuf", [CH, 2 * HALO], "bfloat16"),
    "hL": ("sbuf", [CH, 2 * HALO], "bfloat16"),
    "hR": ("sbuf", [CH, 2 * HALO], "bfloat16"),
    "yeL": ("sbuf", [CH, 2 * HALO], "bfloat16"),
    "yeR": ("sbuf", [CH, 2 * HALO], "bfloat16"),
    "ws": ("sbuf", [CH, 3 * CH], "bfloat16"),
    "xs": ("sbuf", [CH, WID], "bfloat16"),
    "pL": ("psum", [CH, BANK], "float32"),
    "pR": ("psum", [CH, BANK], "float32"),
}
SEMAPHORES = ["ld_edge", "sent", "arrL", "arrR", "ld_w", "mmL", "mmR", "cpL", "cpR", "st_a", "st_b"]
for _j in range(NP):
    SCRATCH["yc%d" % _j] = ("sbuf", [CH, HI[_j] - LO[_j]], "bfloat16")
    SCRATCH["pc%d" % _j] = ("psum", [CH, BANK], "float32")
    SEMAPHORES += ["ld_x%d" % _j, "mm%d" % _j, "cp%d" % _j]


def _half(mask, k):
    bits = [1 << b for b in range(mask.bit_length()) if (mask >> b) & 1]
    n = len(bits) // 2
    return sum(bits[0:n] if k == 0 else bits[n:2 * n]), n


def rank_program(g, core, T, topo):
    rank = T.rank_of(core)
    if rank is None:
        return
    S = T.sem
    n_ranks = len(T.cores)
    left = T.cores[rank - 1] if rank > 0 else None
    right = T.cores[rank + 1] if rank + 1 < n_ranks else None
    qa, qb = g.sync, g.scalar
    w = [T.ws[:, CH * i:CH * (i + 1)] for i in range(3)]

    qa.dma_start(T.sL[:, :], T.x[:, 0:2 * HALO]).then_inc(S.ld_edge, 16)
    qb.dma_start(T.sR[:, :], T.x[:, WID - 2 * HALO:WID]).then_inc(S.ld_edge, 16)
    qa.dma_start(T.ws[:, :], T.w[:, :]).then_inc(S.ld_w, 16)
    for j in range(NP):
        q = qb if j % 2 == 0 else qa
        q.dma_start(T.xs[:, CUTS[j]:CUTS[j + 1]], T.x[:, CUTS[j]:CUTS[j + 1]]).then_inc(S["ld_x%d" % j], 16)

    transfers, n_sent, n_arr = [], 0, {}
    for side, dst, src_ap, dst_ap, sem in (("L", left, T.sL[:, 0:HALO], T.hR[:, 0:HALO], S.arrR),
                                           ("R", right, T.sR[:, HALO:2 * HALO], T.hL[:, 0:HALO], S.arrL)):
        if dst is None:
            continue
        rid, pid = topo.addr(dst, core)
        m, n = _half(topo.mask(core, dst), len(transfers))
        n_sent += n
        n_arr[side] = _half(topo.mask(dst, core), 0)[1]
        transfers.append(RemoteDMATransfer(dst_ids=[DstId(rid=rid, pnc=pid)], dma_engine_mask=m, remote_sem=sem,
                                           src=src_ap, dst=dst_ap))
    g.wait_ge(S.ld_edge, 32)
    g.remote_dma_fused(transfers, local_sem=S.sent)
    g.wait_ge(S.sent, n_sent)

    te = g.tensor
    eL = T.pL[:, 0:HALO]
    eR = T.pR[:, 0:HALO]
    te.wait_ge(S.ld_w, 16)
    te.wait_ge(S.ld_edge, 32)
    te.matmul(eL, w[1], T.sL[:, 0:HALO], start=True, stop=False)
    mm = te.matmul(eL, w[2], T.sL[:, HALO:2 * HALO], start=False, stop=(left is None))
    if left is None:
        mm.then_inc(S.mmL, 1)
    te.matmul(eR, w[0], T.sR[:, 0:HALO], start=True, stop=False)
    mm = te.matmul(eR, w[1], T.sR[:, HALO:2 * HALO], start=False, stop=(right is None))
    if right is None:
        mm.then_inc(S.mmR, 1)
    for j in range(NP):
        te.wait_ge(S["ld_x%d" % j], 16)
        n = HI[j] - LO[j]
        for i in range(3):
            a = LO[j] + HALO * (i - 1)
            mm = te.matmul(T["pc%d" % j][:, 0:n], w[i], T.xs[:, a:a + n], start=(i == 0), stop=(i == 2))
        mm.then_inc(S["mm%d" % j], 1)
    if right is not None:
        te.wait_ge(S.arrR, n_arr["R"])
        te.matmul(eR, w[2], T.hR[:, 0:HALO], start=False, stop=True).then_inc(S.mmR, 1)
    if left is not None:
        te.wait_ge(S.arrL, n_arr["L"])
        te.matmul(eL, w[0], T.hL[:, 0:HALO], start=False, stop=True).then_inc(S.mmL, 1)

    ve = g.vector
    for j in range(NP):
        ve.wait_ge(S["mm%d" % j], 1)
        ve.tensor_copy(T["yc%d" % j][:, :], T["pc%d" % j][:, 0:HI[j] - LO[j]]).then_inc(S["cp%d" % j], 1)
    ve.wait_ge(S.mmR, 1)
    ve.tensor_copy(T.yeR[:, 0:HALO], eR).then_inc(S.cpR, 1)
    ve.wait_ge(S.mmL, 1)
    ve.tensor_copy(T.yeL[:, 0:HALO], eL).then_inc(S.cpL, 1)

    n_st = {"a": 0, "b": 0}
    for j in range(NP):
        q, key = (qa, "a") if j % 2 == 0 else (qb, "b")
        q.wait_ge(S["cp%d" % j], 1)
        q.dma_start(T.y[:, LO[j]:HI[j]], T["yc%d" % j][:, :]).then_inc(S["st_" + key], 16)
        n_st[key] += 16
    qb.wait_ge(S.cpR, 1)
    qb.dma_start(T.y[:, WID - HALO:WID], T.yeR[:, 0:HALO]).then_inc(S.st_b, 16)
    qa.wait_ge(S.cpL, 1)
    qa.dma_start(T.y[:, 0:HALO], T.yeL[:, 0:HALO]).then_inc(S.st_a, 16)
    qa.wait_ge(S.st_a, n_st["a"] + 16)
    qb.wait_ge(S.st_b, n_st["b"] + 16)
